import numpy as np
import ml_dtypes


def mxq(x, axis, fmt="e4m3"):
    dtype, down = {"e4m3": (ml_dtypes.float8_e4m3fn, 7), "e5m2": (ml_dtypes.float8_e5m2, 14)}[fmt]
    v = np.moveaxis(np.asarray(x, np.float32).astype(ml_dtypes.bfloat16).astype(np.float64), axis, -1)
    blocks = v.reshape(v.shape[:-1] + (-1, 32))
    amax = np.abs(blocks).max(-1, keepdims=True)
    byte = np.maximum(np.where(amax > 0, np.frexp(amax)[1] - 1 + 127, 0) - down, 1)
    scale = np.exp2(byte - 127.0)
    codes = (blocks / scale).astype(np.float32).astype(dtype).astype(np.float64)
    return np.moveaxis((codes * scale).reshape(v.shape), -1, axis)


WIDE = False


def mx_kscale(k):
    if not WIDE:
        return np.ones(k)
    levels = np.array([10, -10, 5, -5, 0])
    if k % 512:
        return np.exp2(np.random.permutation(np.resize(levels, k // 32))).repeat(32)
    a = np.empty((k // 512, 16))
    for p in range(k // 512):
        a[p, :8] = np.random.permutation(np.resize(levels, 8))
        for g in range(8):
            far = levels[np.abs(levels - a[p, g]) >= 10]
            a[p, g + 8] = far[np.random.randint(len(far))]
    return np.exp2(a.ravel()).repeat(32)


def f64(x):
    return np.asarray(x).astype(np.float64)


def striped(idx):
    return np.tile(np.asarray(idx).reshape(-1, 16).T, (8, 1)).astype(np.uint16)


def unstriped(offs):
    return offs[:16].T.reshape(-1).astype(np.int64)


def striped8(idx):
    return np.asarray(idx).reshape(8, -1, 16).transpose(0, 2, 1).reshape(128, -1).astype(np.uint16)


def unstriped8(offs):
    return offs.reshape(8, 16, -1).transpose(0, 2, 1).reshape(8, -1).astype(np.int64)


def pick8(x, idx, run):
    r = np.arange(len(x))
    return x[r[:, None], idx[r % (8 * run) // run]]


E2M1 = np.array([0.0, 0.5, 1.0, 1.5, 2.0, 3.0, 4.0, 6.0, -0.0, -0.5, -1.0, -1.5, -2.0, -3.0, -4.0, -6.0])


def pack_weight(w, fmt):
    k, n = w.shape
    w = f64(np.asarray(w, np.float32).astype(ml_dtypes.bfloat16)).reshape(k // 32, 32, n)
    amax = np.abs(w).max(1)
    if fmt == "e4m3":
        byte = np.frexp(amax)[1] - 1 + 127 - 7
    else:
        mant, ex = np.frexp(amax / 6.0)
        byte = np.where(mant > 0.5, ex, ex - 1) + 127
    byte = np.clip(np.where(amax > 0, byte, 1), 1, 254)
    scaled = (w * np.exp2(127.0 - byte)[:, None, :]).reshape(k, n).astype(np.float32)
    by_word = np.ascontiguousarray(scaled.reshape(k // 512, 128, 4, n).transpose(0, 1, 3, 2))
    if fmt == "e4m3":
        words = by_word.astype(ml_dtypes.float8_e4m3fn).view(np.uint8)
    else:
        c = by_word.astype(ml_dtypes.float4_e2m1fn).view(np.uint8) & 0xF
        words = (c[..., 0::2] | (c[..., 1::2] << 4)).reshape(k // 512, 128, 2 * n)
    return np.ascontiguousarray(words), np.ascontiguousarray(byte.astype(np.uint8).reshape(k // 512, 16, n))


def unpack_weight(words, scales, fmt):
    g, _, n = scales.shape
    words = np.ascontiguousarray(words).reshape(g, 128, n, -1)
    if fmt == "e4m3":
        vals = words.view(ml_dtypes.float8_e4m3fn).astype(np.float64)
    else:
        nib = np.empty((g, 128, n, 4), np.uint8)
        nib[..., 0::2] = words & 0xF
        nib[..., 1::2] = words >> 4
        vals = E2M1[nib]
    vals = vals * np.repeat(np.exp2(scales.astype(np.float64) - 127.0), 8, axis=1)[..., None]
    return vals.transpose(0, 1, 3, 2).reshape(g * 512, n)


def bf(x):
    return np.asarray(x, np.float32).astype(ml_dtypes.bfloat16)


def planes(Y):
    r, m = Y.shape
    b = f64(bf(Y)).reshape(r // 32, 32, m)
    amax = np.abs(b).max(1)
    byte = np.clip(np.where(amax > 0, np.frexp(amax)[1] - 1 + 127 - 7, 1), 1, 254)
    codes = (b * np.exp2(127.0 - byte)[:, None, :]).reshape(r, m).astype(np.float32).astype(ml_dtypes.float8_e4m3fn).view(np.uint8)
    words = codes.reshape(r // 512, 128, 4, m).transpose(0, 1, 3, 2)
    return np.ascontiguousarray(words), np.ascontiguousarray(byte.astype(np.uint8).reshape(r // 512, 16, m))


D, T, U, V, I, Q, E = 512, 2048, 512, 1024, 512, 256, 512


def setup_inputs():
    n = np.random.standard_normal
    idx = np.stack([np.random.permutation(T)[:I] for _ in range(8)])
    idx2 = np.random.randint(0, U, I)
    idx3 = np.random.permutation(V)[:I]
    fd = mx_kscale(D)
    fi = mx_kscale(I)
    ti = np.ones(V)
    ti[idx3] = fi
    piecep = pack_weight(n((D, T)) / fd[:, None], "e4m3")
    return {
        "query": (n((D, Q)) * 0.25 / np.sqrt(D) * fd[:, None]).astype(np.float32),
        "piece_words": piecep[0],
        "piece_scales": piecep[1],
        "cent": (n((D, U)) / fd[:, None]).astype(np.float32),
        "trust": (np.random.uniform(0.5, 1.2, (Q, 1))).astype(np.float32),
        "size": (np.random.uniform(0.5, 2.0, (1, I)) * fi).astype(np.float32),
        "vals": (n((E, V)) / ti).astype(np.float32),
        "offs": striped8(idx),
        "offs2": striped(idx2),
        "offs3": striped(idx3),
    }


def reference(query, piece_words, piece_scales, cent, trust, size, vals, offs, offs2, offs3):
    idx = unstriped8(offs)
    idx2 = unstriped(offs2)
    idx3 = unstriped(offs3)
    pieceu = unpack_weight(piece_words, piece_scales, "e4m3")
    queryq = mxq(f64(query), 0, "e4m3")
    pieceidxg = pick8(pieceu, idx, 64)
    a = queryq.T @ pieceidxg
    centq = mxq(f64(cent), 0, "e4m3")
    b = queryq.T @ centq
    s = a + b[:, idx2] * f64(trust)
    p = np.exp(s - np.max(s, axis=1, keepdims=True))
    w = p * f64(size) / np.sum(p, axis=1, keepdims=True)
    wt = w.T
    vt = f64(vals)[:, idx3].T
    vtq = mxq(vt, 0, "e4m3")
    wtq = mxq(wt, 0, "e4m3")
    o = vtq.T @ wtq
    words, scales = planes(o)
    return o, words, scales

@@ -1,0 +1,348 @@
+from contextlib import ExitStack
+
+import concourse.mybir as mybir
+from concourse.masks import make_identity
+
+F32 = mybir.dt.float32
+BF16 = mybir.dt.bfloat16
+I32 = mybir.dt.int32
+U32 = mybir.dt.uint32
+U16 = mybir.dt.uint16
+U8 = mybir.dt.uint8
+FP8X4 = mybir.dt.float8_e4m3fn_x4
+ALU = mybir.AluOpType
+ACT = mybir.ActivationFunctionType
+AXIS = mybir.AxisListType
+
+P = 128
+PACK = 4
+D, T, U, V, SLOTS, Q, E = 512, 2048, 512, 1024, 512, 256, 512
+Q_TILES = Q // P
+BASE_WINDOW = 704
+HALF = U // 2
+SPLIT = 160
+
+FLOPS = 2 * Q * D * SLOTS + 2 * Q * D * U + 2 * E * SLOTS * Q
+
+
+def interleave(engine_copy, grouped, raw):
+    engine_copy(
+        out=grouped.rearrange("p (c i) t -> p c t i", i=PACK),
+        in_=raw.rearrange("p t (c i) -> p c t i", i=PACK),
+    )
+
+
+def tile_attend_compositebase_pl_kernel(
+    tc, query, piece_words, piece_scales, cent, trust, size, vals, offs, offs2, offs3, out_0, out_1, out_2
+):
+    nc = tc.nc
+
+    def quantize(codes, scales, grouped):
+        nc.vector.quantize_mx(out=codes.bitcast(FP8X4), scales=scales, in_=grouped.rearrange("p c t -> p (c t)"))
+
+    def product(out, lhs_codes, lhs_scales, rhs_codes, rhs_scales):
+        nc.tensor.matmul_mx(
+            out=out, lhsT=lhs_codes.bitcast(FP8X4), lhsT_scale=lhs_scales,
+            rhs=rhs_codes.bitcast(FP8X4), rhs_scale=rhs_scales, start=True, stop=True,
+        )
+
+    with ExitStack() as ctx:
+        sb = ctx.enter_context(tc.tile_pool(name="sb", bufs=1))
+        ps = ctx.enter_context(tc.psum_pool(name="ps", bufs=1))
+
+        def tile(shape, dtype, name, tag=None):
+            return sb.tile(shape, dtype, name=name, tag=tag or name, align_bytes=64)
+
+        piece_list = sb.tile([P, SLOTS // 16], U16, name="piece_list")
+        base_list = sb.tile([P, SLOTS // 16], U16, name="base_list")
+        value_list = sb.tile([P, SLOTS // 16], U16, name="value_list")
+        store_bytes = tile([P, T], U8, "store_bytes")
+        warm = tile([P, 1], F32, "warm")
+        store_words = tile([P, T], I32, "store_words")
+        query_raw = tile([P, PACK, Q], F32, "query_raw", "raw1")
+        cent_raw = [tile([P, PACK, HALF], F32, "cent_raw%d" % h, "raw%d" % (h + 2)) for h in range(2)]
+        vals_raw = {0: tile([P, V], F32, "vals_raw0")}
+        trust_cols = tile([P, Q_TILES], F32, "trust_cols")
+        size_cols = tile([P, PACK], F32, "size_cols")
+        cent_rows = cent.rearrange("(p t) u -> p t u", t=PACK)
+        vals_rows = vals.rearrange("(p j) v -> p j v", j=PACK)
+
+        nc.gpsimd.memset(warm[:], 0.0)
+        nc.scalar.activation(out=warm[:], in_=warm[:], func=ACT.Exp)
+        nc.sync.dma_start(piece_list[:], offs)
+        nc.sync.dma_start(
+            out=store_bytes[:].bitcast(I32),
+            in_=piece_scales[0].bitcast(I32).unsqueeze(1).to_broadcast([16, 8, T // 4]),
+        )
+        nc.sync.dma_start(out=query_raw[:], in_=query.rearrange("(p t) q -> p t q", t=PACK))
+        for h in range(2):
+            nc.sync.dma_start(out=cent_raw[h][:], in_=cent_rows[:, :, h * HALF : (h + 1) * HALF])
+        nc.sync.dma_start(value_list[:], offs3)
+        nc.sync.dma_start(base_list[:], offs2)
+        nc.sync.dma_start(out=vals_raw[0][:], in_=vals_rows[:, 0, :])
+        nc.sync.dma_start(out=size_cols[:], in_=size.rearrange("o (p t) -> p (o t)", t=PACK))
+        with nc.allow_non_contiguous_dma(reason="one trust value a partition"):
+            nc.sync.dma_start(out=trust_cols[:], in_=trust.rearrange("(c p) o -> p (c o)", p=P))
+        nc.sync.dma_start(out=store_words[:], in_=piece_words[0].rearrange("p c t -> p (c t)").bitcast(I32))
+
+        ident = tile([P, P], F32, "ident")
+        make_identity(nc, ident[:])
+        key_scales = tile([P, SLOTS], U8, "key_scales")
+        nc.gpsimd.memset(key_scales[:].bitcast(I32), 0)
+        base_scores = [tile([P, BASE_WINDOW], F32, "base_scores%d" % c) for c in range(Q_TILES)]
+        for c in range(Q_TILES):
+            nc.gpsimd.memset(base_scores[c][:, U:], 0.0)
+
+        picked_bytes = tile([P, SLOTS], U8, "picked_bytes")
+        cent_codes = [tile([P, HALF], U32, "cent_codes%d" % h) for h in range(2)]
+        cent_scales = [tile([P, HALF], U8, "cent_scales%d" % h) for h in range(2)]
+        cent_grouped = [tile([P, HALF, PACK], BF16, "cent_grouped%d" % h) for h in range(2)]
+        query_grouped = tile([P, Q, PACK], BF16, "query_grouped")
+        query_codes = tile([P, Q], U32, "query_codes")
+        query_scales = tile([P, Q], U8, "query_scales")
+        value_grouped = {}
+        value_codes = {}
+        value_scales = [tile([P, P], U8, "value_scales%d" % j) for j in range(PACK)]
+        result_codes = tile([P, Q], U32, "result_codes")
+        result_scales = tile([P, Q], U8, "result_scales")
+        out_rows = out_0.rearrange("(p j) q -> p j q", j=PACK)
+        out_words = out_1[0].rearrange("p c t -> p (c t)").bitcast(I32)
+        t = {}
+        copy_on = {"V": nc.vector.tensor_copy, "S": nc.scalar.copy}
+
+        def qcols(c):
+            return slice(c * P, (c + 1) * P)
+
+        def gby():
+            nc.vector.tensor_copy(picked_bytes[:], store_bytes[:].indirect(piece_list[:]))
+
+        def mv():
+            for x in range(4):
+                nc.sync.dma_start(
+                    out=key_scales[32 * x : 32 * x + 4, :].bitcast(I32),
+                    in_=picked_bytes[32 * x : 32 * x + 32 : 8, :].bitcast(I32),
+                )
+
+        def ts():
+            t["size_bank"] = ps.tile([P, PACK, P], F32, name="size_bank", tag="base01")
+            for k in range(PACK):
+                nc.tensor.transpose(t["size_bank"][:, k, :], size_cols[:, k : k + 1].to_broadcast([P, P]), ident[:])
+
+        def cq():
+            interleave(nc.vector.tensor_copy, query_grouped[:], query_raw[:])
+
+        def qq():
+            quantize(query_codes[:], query_scales[:], query_grouped[:])
+
+        def ccv(h):
+            interleave(nc.vector.tensor_copy, cent_grouped[h][:, 0:SPLIT, :], cent_raw[h][:, :, 0:SPLIT])
+
+        def ccs(h):
+            interleave(nc.scalar.copy, cent_grouped[h][:, SPLIT:HALF, :], cent_raw[h][:, :, SPLIT:HALF])
+
+        def qc(h):
+            quantize(cent_codes[h][:], cent_scales[h][:], cent_grouped[h][:])
+
+        def lv(j):
+            vals_raw[j] = tile([P, V], F32, "vals_raw%d" % j, "raw%d" % j)
+            nc.sync.dma_start(out=vals_raw[j][:], in_=vals_rows[:, j, :])
+
+        def mb(c, h):
+            t["b", c, h] = ps.tile([P, HALF], F32, name="base_bank%d%d" % (c, h), tag="base%d%d" % (c, h))
+            product(t["b", c, h][:], query_codes[:, qcols(c)], query_scales[:, qcols(c)], cent_codes[h][:], cent_scales[h][:])
+
+        def cb(c, h):
+            nc.scalar.copy(out=base_scores[c][:, h * HALF : (h + 1) * HALF], in_=t["b", c, h][:])
+
+        def gv(j, tag=None):
+            t["pv", j] = tile([P, SLOTS], BF16, "picked_vals%d" % j, tag)
+            nc.vector.tensor_copy(t["pv", j][:], vals_raw[j][:].indirect(value_list[:]))
+
+        def cv(j, tag=None):
+            t["vh", j] = tile([P, V], BF16, "vals_half%d" % j, tag)
+            nc.scalar.activation(out=t["vh", j][:], in_=vals_raw[j][:], func=ACT.Copy)
+
+        def sv(j, tag=None):
+            t["pv", j] = tile([P, SLOTS], BF16, "picked_vals%d" % j, tag)
+            nc.scalar.activation(out=t["pv", j][:], in_=t["vh", j][:].indirect(value_list[:]), func=ACT.Copy)
+
+        def tv(j):
+            t["vb", j] = ps.tile([P, 2, P], F32, name="value_bank%d" % j, tag=["base11", "piece0", "base11", "piece1"][j])
+            pairs = t["pv", j][:].bitcast(F32)
+            for u in range(2):
+                nc.tensor.transpose(t["vb", j][:, u, :], pairs[:, u::2], ident[:])
+
+        def xv(j, e, tag=None):
+            value_grouped[j] = tile([P, P, PACK], BF16, "value_grouped%d" % j, tag)
+            copy_on[e](
+                out=value_grouped[j][:].rearrange("s c t -> s (c t)").bitcast(F32).rearrange("s (p u) -> s p u", u=2),
+                in_=t["vb", j][:].rearrange("s u p -> s p u"),
+            )
+
+        def qv(j, tag=None):
+            value_codes[j] = tile([P, P], U32, "value_codes%d" % j, tag)
+            quantize(value_codes[j][:], value_scales[j][:], value_grouped[j][:])
+
+        def gw(tag=None):
+            t["key_codes"] = tile([P, SLOTS], U32, "key_codes", tag)
+            nc.vector.tensor_copy(t["key_codes"][:], store_words[:].bitcast(U32).indirect(piece_list[:]))
+
+        def ma(c):
+            t["a", c] = ps.tile([P, SLOTS], F32, name="piece_bank%d" % c, tag="piece%d" % c)
+            product(t["a", c][:], query_codes[:, qcols(c)], query_scales[:, qcols(c)], t["key_codes"][:], key_scales[:])
+
+        def gb(c, tag=None):
+            t["g", c] = tile([P, SLOTS], F32, "picked_base%d" % c, tag)
+            nc.vector.tensor_copy(t["g", c][:], base_scores[c][:].indirect(base_list[:]))
+
+        def s(c):
+            t["s", c] = tile([P, SLOTS], F32, "scores%d" % c)
+            nc.vector.scalar_tensor_tensor(
+                out=t["s", c][:], in0=t["g", c][:], scalar=trust_cols[:, c : c + 1], in1=t["a", c][:],
+                op0=ALU.mult, op1=ALU.add,
+            )
+
+        def m(c, tag=None):
+            t["m", c] = tile([P, 1], F32, "neg_max%d" % c, tag)
+            nc.vector.tensor_reduce(out=t["m", c][:], in_=t["s", c][:], axis=AXIS.X, op=ALU.max, negate=True)
+
+        def e(c):
+            t["p", c] = tile([P, SLOTS], F32, "probs%d" % c)
+            t["sum", c] = tile([P, 1], F32, "row_sum%d" % c)
+            nc.scalar.activation(out=t["p", c][:], in_=t["s", c][:], func=ACT.Exp, bias=t["m", c][:], accum_out=t["sum", c][:])
+
+        def r(c, tag=None):
+            t["r", c] = tile([P, 1], F32, "inv_sum%d" % c, tag)
+            nc.vector.reciprocal(out=t["r", c][:], in_=t["sum", c][:])
+
+        def w(c):
+            t["w", c] = tile([P, SLOTS], BF16, "w_rows%d" % c)
+            nc.vector.scalar_tensor_tensor(
+                out=t["w", c][:].rearrange("q (s t) -> q s t", t=PACK),
+                in0=t["p", c][:].rearrange("q (s t) -> q s t", t=PACK),
+                scalar=t["r", c][:],
+                in1=t["size_bank"][:].rearrange("q t s -> q s t"),
+                op0=ALU.mult, op1=ALU.mult,
+            )
+
+        def tw(c):
+            t["wb", c] = ps.tile([P, 2, P], F32, name="weight_bank%d" % c, tag="weight%d" % c)
+            pairs = t["w", c][:].bitcast(F32)
+            for u in range(2):
+                nc.tensor.transpose(t["wb", c][:, u, :], pairs[:, u::2], ident[:])
+
+        def cw(c, e):
+            t["wg", c] = tile([P, P, PACK], BF16, "weight_grouped%d" % c)
+            copy_on[e](
+                out=t["wg", c][:].rearrange("s q t -> s (q t)").bitcast(F32).rearrange("s (q u) -> s q u", u=2),
+                in_=t["wb", c][:].rearrange("s u q -> s q u"),
+            )
+
+        def qw(c):
+            t["wc", c] = tile([P, P], U32, "weight_codes%d" % c)
+            t["ws", c] = tile([P, P], U8, "weight_scales%d" % c)
+            quantize(t["wc", c][:], t["ws", c][:], t["wg", c][:])
+
+        def mo(c, order):
+            if ("o", c) not in t:
+                t["o", c] = ps.tile([P, PACK, P], F32, name="result_bank%d" % c, tag="base%d0" % c)
+            for j in order:
+                product(t["o", c][:, j, :], value_codes[j][:], value_scales[j][:], t["wc", c][:], t["ws", c][:])
+
+        def ob(c, from_sbuf=False):
+            t["og", c] = tile([P, P, PACK], BF16, "result_grouped%d" % c)
+            if from_sbuf:
+                interleave(nc.vector.tensor_copy, t["og", c][:], t["res", c][:])
+            else:
+                nc.vector.tensor_copy(out=t["og", c][:], in_=t["o", c][:].rearrange("p j q -> p q j"))
+
+        def of(c):
+            result = tile([P, PACK, P], F32, "result%d" % c)
+            t["res", c] = result
+            nc.scalar.copy(out=result[:], in_=t["o", c][:])
+            nc.sync.dma_start(out=out_rows[:, :, qcols(c)], in_=result[:])
+
+        def qo(c):
+            quantize(result_codes[:, qcols(c)], result_scales[:, qcols(c)], t["og", c][:])
+
+        def sw():
+            nc.sync.dma_start(out=out_words, in_=result_codes[:].bitcast(I32))
+            for x in range(4):
+                queue = nc.sync if x % 2 == 0 else nc.scalar
+                queue.dma_start(
+                    out=out_2[0, 4 * x : 4 * x + 4, :].bitcast(I32),
+                    in_=result_scales[32 * x : 32 * x + 4, :].bitcast(I32),
+                )
+
+        gby()
+        mv()
+        cq()
+        lv(1)
+        ccv(0)
+        ccs(0)
+        qq()
+        qc(0)
+        lv(2)
+        ccv(1)
+        ccs(1)
+        lv(3)
+        mb(0,0)
+        mb(1,0)
+        qc(1)
+        cb(0,0)
+        cb(1,0)
+        gv(0,"cent_grouped1")
+        mb(0,1)
+        mb(1,1)
+        cb(0,1)
+        cb(1,1)
+        ts()
+        tv(0)
+        gb(0)
+        xv(0,"S")
+        gw()
+        cv(1,"base_scores0")
+        gb(1,"store_words")
+        ma(0)
+        cv(2,"cent_grouped1")
+        ma(1)
+        s(0)
+        s(1)
+        sv(1,"raw2")
+        m(0)
+        m(1)
+        e(0)
+        gv(3,"store_words")
+        tv(1)
+        e(1)
+        sv(2,"scores1")
+        r(0,"raw3")
+        r(1)
+        tv(3)
+        w(0)
+        w(1)
+        tw(0)
+        xv(1,"V","probs0")
+        xv(3,"V","raw3")
+        tw(1)
+        cw(0,"S")
+        tv(2)
+        qv(0,"probs1")
+        qv(1)
+        qw(0)
+        qv(3)
+        cw(1,"S")
+        xv(2,"S")
+        mo(0,[0,1,3])
+        qw(1)
+        qv(2)
+        mo(1,[0,1,3])
+        mo(0,[2])
+        mo(1,[2])
+        of(0)
+        ob(1)
+        ob(0,True)
+        of(1)
+        qo(1)
+        qo(0)
+        sw()

@@ -20,7 +20,6 @@ D, T, U, V, SLOTS, Q, E = 512, 2048, 512, 1024, 512, 256, 512
 Q_TILES = Q // P
 BASE_WINDOW = 704
 HALF = U // 2
-SPLIT = 160
 
 FLOPS = 2 * Q * D * SLOTS + 2 * Q * D * U + 2 * E * SLOTS * Q
 
@@ -59,14 +58,17 @@ def tile_attend_compositebase_pl_kernel(
         store_bytes = tile([P, T], U8, "store_bytes")
         warm = tile([P, 1], F32, "warm")
         store_words = tile([P, T], I32, "store_words")
-        query_raw = tile([P, PACK, Q], F32, "query_raw", "raw1")
-        cent_raw = [tile([P, PACK, HALF], F32, "cent_raw%d" % h, "raw%d" % (h + 2)) for h in range(2)]
-        vals_raw = {0: tile([P, V], F32, "vals_raw0")}
+        query_raw = tile([P, PACK, Q], F32, "query_raw", "raw2")
+        cent_raw = [tile([P, PACK, HALF], F32, "cent_raw%d" % h, "raw%d" % (h + 3)) for h in range(2)]
+        vals_raw = {j: tile([P, V], F32, "vals_raw%d" % j) for j in range(2)}
         trust_cols = tile([P, Q_TILES], F32, "trust_cols")
         size_cols = tile([P, PACK], F32, "size_cols")
         cent_rows = cent.rearrange("(p t) u -> p t u", t=PACK)
         vals_rows = vals.rearrange("(p j) v -> p j v", j=PACK)
 
+        nc.scalar.dma_start(out=size_cols[:], in_=size.rearrange("o (p t) -> p (o t)", t=PACK))
+        with nc.allow_non_contiguous_dma(reason="one trust value a partition"):
+            nc.scalar.dma_start(out=trust_cols[:], in_=trust.rearrange("(c p) o -> p (c o)", p=P))
         nc.gpsimd.memset(warm[:], 0.0)
         nc.scalar.activation(out=warm[:], in_=warm[:], func=ACT.Exp)
         nc.sync.dma_start(piece_list[:], offs)
@@ -80,9 +82,7 @@ def tile_attend_compositebase_pl_kernel(
         nc.sync.dma_start(value_list[:], offs3)
         nc.sync.dma_start(base_list[:], offs2)
         nc.sync.dma_start(out=vals_raw[0][:], in_=vals_rows[:, 0, :])
-        nc.sync.dma_start(out=size_cols[:], in_=size.rearrange("o (p t) -> p (o t)", t=PACK))
-        with nc.allow_non_contiguous_dma(reason="one trust value a partition"):
-            nc.sync.dma_start(out=trust_cols[:], in_=trust.rearrange("(c p) o -> p (c o)", p=P))
+        nc.sync.dma_start(out=vals_raw[1][:], in_=vals_rows[:, 1, :])
         nc.sync.dma_start(out=store_words[:], in_=piece_words[0].rearrange("p c t -> p (c t)").bitcast(I32))
 
         ident = tile([P, P], F32, "ident")
@@ -129,16 +129,13 @@ def tile_attend_compositebase_pl_kernel(
                 nc.tensor.transpose(t["size_bank"][:, k, :], size_cols[:, k : k + 1].to_broadcast([P, P]), ident[:])
 
         def cq():
-            interleave(nc.vector.tensor_copy, query_grouped[:], query_raw[:])
+            interleave(nc.scalar.copy, query_grouped[:], query_raw[:])
 
         def qq():
             quantize(query_codes[:], query_scales[:], query_grouped[:])
 
         def ccv(h):
-            interleave(nc.vector.tensor_copy, cent_grouped[h][:, 0:SPLIT, :], cent_raw[h][:, :, 0:SPLIT])
-
-        def ccs(h):
-            interleave(nc.scalar.copy, cent_grouped[h][:, SPLIT:HALF, :], cent_raw[h][:, :, SPLIT:HALF])
+            interleave(nc.vector.tensor_copy, cent_grouped[h][:], cent_raw[h][:])
 
         def qc(h):
             quantize(cent_codes[h][:], cent_scales[h][:], cent_grouped[h][:])
@@ -167,7 +164,7 @@ def tile_attend_compositebase_pl_kernel(
             nc.scalar.activation(out=t["pv", j][:], in_=t["vh", j][:].indirect(value_list[:]), func=ACT.Copy)
 
         def tv(j):
-            t["vb", j] = ps.tile([P, 2, P], F32, name="value_bank%d" % j, tag=["base11", "piece0", "base11", "piece1"][j])
+            t["vb", j] = ps.tile([P, 2, P], F32, name="value_bank%d" % j, tag=["base11", "weight0", "piece0", "piece1"][j])
             pairs = t["pv", j][:].bitcast(F32)
             for u in range(2):
                 nc.tensor.transpose(t["vb", j][:, u, :], pairs[:, u::2], ident[:])
@@ -206,8 +203,8 @@ def tile_attend_compositebase_pl_kernel(
             t["m", c] = tile([P, 1], F32, "neg_max%d" % c, tag)
             nc.vector.tensor_reduce(out=t["m", c][:], in_=t["s", c][:], axis=AXIS.X, op=ALU.max, negate=True)
 
-        def e(c):
-            t["p", c] = tile([P, SLOTS], F32, "probs%d" % c)
+        def e(c, tag=None):
+            t["p", c] = tile([P, SLOTS], F32, "probs%d" % c, tag)
             t["sum", c] = tile([P, 1], F32, "row_sum%d" % c)
             nc.scalar.activation(out=t["p", c][:], in_=t["s", c][:], func=ACT.Exp, bias=t["m", c][:], accum_out=t["sum", c][:])
 
@@ -264,9 +261,9 @@ def tile_attend_compositebase_pl_kernel(
 
         def qo(c):
             quantize(result_codes[:, qcols(c)], result_scales[:, qcols(c)], t["og", c][:])
+            nc.sync.dma_start(out=out_words[:, qcols(c)], in_=result_codes[:, qcols(c)].bitcast(I32))
 
         def sw():
-            nc.sync.dma_start(out=out_words, in_=result_codes[:].bitcast(I32))
             for x in range(4):
                 queue = nc.sync if x % 2 == 0 else nc.scalar
                 queue.dma_start(
@@ -277,15 +274,12 @@ def tile_attend_compositebase_pl_kernel(
         gby()
         mv()
         cq()
-        lv(1)
+        lv(2)
         ccv(0)
-        ccs(0)
+        lv(3)
         qq()
         qc(0)
-        lv(2)
         ccv(1)
-        ccs(1)
-        lv(3)
         mb(0,0)
         mb(1,0)
         qc(1)
@@ -296,53 +290,51 @@ def tile_attend_compositebase_pl_kernel(
         mb(1,1)
         cb(0,1)
         cb(1,1)
+        cv(1,"cent_scales1")
         ts()
+        gb(0,"vals_raw0")
+        sv(1)
         tv(0)
-        gb(0)
+        gw("cent_codes1")
         xv(0,"S")
-        gw()
-        cv(1,"base_scores0")
+        tv(1)
+        cv(2,"cent_scales1")
         gb(1,"store_words")
         ma(0)
-        cv(2,"cent_grouped1")
         ma(1)
+        sv(2)
         s(0)
         s(1)
-        sv(1,"raw2")
         m(0)
+        tv(2)
         m(1)
-        e(0)
+        e(0,"cent_scales1")
         gv(3,"store_words")
-        tv(1)
         e(1)
-        sv(2,"scores1")
+        xv(1,"S","scores0")
+        xv(2,"S","scores1")
         r(0,"raw3")
         r(1)
         tv(3)
         w(0)
+        xv(3,"S","neg_max1")
         w(1)
         tw(0)
-        xv(1,"V","probs0")
-        xv(3,"V","raw3")
-        tw(1)
+        qv(0,"cent_scales1")
+        qv(1,"raw3")
         cw(0,"S")
-        tv(2)
-        qv(0,"probs1")
-        qv(1)
+        tw(1)
         qw(0)
-        qv(3)
+        qv(2,"probs1")
+        qv(3,"inv_sum1")
         cw(1,"S")
-        xv(2,"S")
-        mo(0,[0,1,3])
+        mo(0,[0,1,2,3])
         qw(1)
-        qv(2)
-        mo(1,[0,1,3])
-        mo(0,[2])
-        mo(1,[2])
+        mo(1,[0,1,2,3])
+        ob(0)
         of(0)
+        qo(0)
         ob(1)
-        ob(0,True)
         of(1)
         qo(1)
-        qo(0)
         sw()

@@ -129,7 +129,7 @@ def tile_attend_compositebase_pl_kernel(
                 nc.tensor.transpose(t["size_bank"][:, k, :], size_cols[:, k : k + 1].to_broadcast([P, P]), ident[:])
 
         def cq():
-            interleave(nc.scalar.copy, query_grouped[:], query_raw[:])
+            interleave(nc.vector.tensor_copy, query_grouped[:], query_raw[:])
 
         def qq():
             quantize(query_codes[:], query_scales[:], query_grouped[:])
@@ -164,7 +164,7 @@ def tile_attend_compositebase_pl_kernel(
             nc.scalar.activation(out=t["pv", j][:], in_=t["vh", j][:].indirect(value_list[:]), func=ACT.Copy)
 
         def tv(j):
-            t["vb", j] = ps.tile([P, 2, P], F32, name="value_bank%d" % j, tag=["base11", "weight0", "piece0", "piece1"][j])
+            t["vb", j] = ps.tile([P, 2, P], F32, name="value_bank%d" % j, tag=["weight0", "base11", "piece0", "piece1"][j])
             pairs = t["pv", j][:].bitcast(F32)
             for u in range(2):
                 nc.tensor.transpose(t["vb", j][:, u, :], pairs[:, u::2], ident[:])
@@ -253,10 +253,10 @@ def tile_attend_compositebase_pl_kernel(
             else:
                 nc.vector.tensor_copy(out=t["og", c][:], in_=t["o", c][:].rearrange("p j q -> p q j"))
 
-        def of(c):
+        def of(c, e):
             result = tile([P, PACK, P], F32, "result%d" % c)
             t["res", c] = result
-            nc.scalar.copy(out=result[:], in_=t["o", c][:])
+            copy_on[e](out=result[:], in_=t["o", c][:])
             nc.sync.dma_start(out=out_rows[:, :, qcols(c)], in_=result[:])
 
         def qo(c):
@@ -275,9 +275,9 @@ def tile_attend_compositebase_pl_kernel(
         mv()
         cq()
         lv(2)
+        qq()
         ccv(0)
         lv(3)
-        qq()
         qc(0)
         ccv(1)
         mb(0,0)
@@ -285,22 +285,23 @@ def tile_attend_compositebase_pl_kernel(
         qc(1)
         cb(0,0)
         cb(1,0)
-        gv(0,"cent_grouped1")
+        cv(0)
+        gv(1,"cent_grouped1")
         mb(0,1)
         mb(1,1)
         cb(0,1)
         cb(1,1)
-        cv(1,"cent_scales1")
         ts()
-        gb(0,"vals_raw0")
-        sv(1)
-        tv(0)
-        gw("cent_codes1")
-        xv(0,"S")
+        sv(0,"cent_scales1")
+        gb(0,"vals_raw1")
         tv(1)
-        cv(2,"cent_scales1")
+        gw("cent_codes1")
+        xv(1,"S")
+        tv(0)
+        cv(2,"vals_half0")
         gb(1,"store_words")
         ma(0)
+        xv(0,"S")
         ma(1)
         sv(2)
         s(0)
@@ -308,19 +309,18 @@ def tile_attend_compositebase_pl_kernel(
         m(0)
         tv(2)
         m(1)
-        e(0,"cent_scales1")
+        e(0,"vals_half0")
         gv(3,"store_words")
         e(1)
-        xv(1,"S","scores0")
-        xv(2,"S","scores1")
+        xv(2,"S","scores0")
         r(0,"raw3")
         r(1)
         tv(3)
         w(0)
-        xv(3,"S","neg_max1")
+        xv(3,"S","scores1")
         w(1)
         tw(0)
-        qv(0,"cent_scales1")
+        qv(0,"vals_half0")
         qv(1,"raw3")
         cw(0,"S")
         tw(1)
@@ -332,9 +332,9 @@ def tile_attend_compositebase_pl_kernel(
         qw(1)
         mo(1,[0,1,2,3])
         ob(0)
-        of(0)
+        of(0,"S")
         qo(0)
         ob(1)
-        of(1)
+        of(1,"V")
         qo(1)
         sw()

@@ -18,23 +18,32 @@ P = 128
 PACK = 4
 D, T, U, V, SLOTS, Q, E = 512, 2048, 512, 1024, 512, 256, 512
 Q_TILES = Q // P
+BLOCKS = D // 32
+QUADRANT = 32
+BLOCK_PARTITIONS = 8
+LIST_COLUMNS = SLOTS // 16
 BASE_WINDOW = 704
 HALF = U // 2
+EARLY_PLANES = 2
+VALUE_BANK_TAGS = ("weight0", "base11", "piece0", "piece1")
 
 FLOPS = 2 * Q * D * SLOTS + 2 * Q * D * U + 2 * E * SLOTS * Q
 
 
-def interleave(engine_copy, grouped, raw):
-    engine_copy(
-        out=grouped.rearrange("p (c i) t -> p c t i", i=PACK),
-        in_=raw.rearrange("p t (c i) -> p c t i", i=PACK),
-    )
+def query_columns(c):
+    return slice(c * P, (c + 1) * P)
 
 
 def tile_attend_compositebase_pl_kernel(
     tc, query, piece_words, piece_scales, cent, trust, size, vals, offs, offs2, offs3, out_0, out_1, out_2
 ):
     nc = tc.nc
+
+    def round_and_group(grouped, raw):
+        nc.vector.tensor_copy(
+            out=grouped.rearrange("p (c i) t -> p c t i", i=PACK),
+            in_=raw.rearrange("p t (c i) -> p c t i", i=PACK),
+        )
 
     def quantize(codes, scales, grouped):
         nc.vector.quantize_mx(out=codes.bitcast(FP8X4), scales=scales, in_=grouped.rearrange("p c t -> p (c t)"))
@@ -49,40 +58,38 @@ def tile_attend_compositebase_pl_kernel(
         sb = ctx.enter_context(tc.tile_pool(name="sb", bufs=1))
         ps = ctx.enter_context(tc.psum_pool(name="ps", bufs=1))
 
-        def tile(shape, dtype, name, tag=None):
-            return sb.tile(shape, dtype, name=name, tag=tag or name, align_bytes=64)
+        def tile(shape, dtype, name, after=None):
+            return sb.tile(shape, dtype, name=name, tag=after or name, align_bytes=64)
 
-        piece_list = sb.tile([P, SLOTS // 16], U16, name="piece_list")
-        base_list = sb.tile([P, SLOTS // 16], U16, name="base_list")
-        value_list = sb.tile([P, SLOTS // 16], U16, name="value_list")
+        piece_list = sb.tile([P, LIST_COLUMNS], U16, name="piece_list")
+        base_list = sb.tile([P, LIST_COLUMNS], U16, name="base_list")
+        value_list = sb.tile([P, LIST_COLUMNS], U16, name="value_list")
         store_bytes = tile([P, T], U8, "store_bytes")
-        warm = tile([P, 1], F32, "warm")
         store_words = tile([P, T], I32, "store_words")
         query_raw = tile([P, PACK, Q], F32, "query_raw", "raw2")
-        cent_raw = [tile([P, PACK, HALF], F32, "cent_raw%d" % h, "raw%d" % (h + 3)) for h in range(2)]
-        vals_raw = {j: tile([P, V], F32, "vals_raw%d" % j) for j in range(2)}
+        cent_raw = [tile([P, PACK, HALF], F32, "cent_raw%d" % h, tag) for h, tag in enumerate(("raw3", "raw4"))]
+        vals_raw = {j: tile([P, V], F32, "vals_raw%d" % j) for j in range(EARLY_PLANES)}
         trust_cols = tile([P, Q_TILES], F32, "trust_cols")
         size_cols = tile([P, PACK], F32, "size_cols")
         cent_rows = cent.rearrange("(p t) u -> p t u", t=PACK)
         vals_rows = vals.rearrange("(p j) v -> p j v", j=PACK)
 
         nc.scalar.dma_start(out=size_cols[:], in_=size.rearrange("o (p t) -> p (o t)", t=PACK))
-        with nc.allow_non_contiguous_dma(reason="one trust value a partition"):
+        with nc.allow_non_contiguous_dma(reason="one trust value a partition and query tile"):
             nc.scalar.dma_start(out=trust_cols[:], in_=trust.rearrange("(c p) o -> p (c o)", p=P))
-        nc.gpsimd.memset(warm[:], 0.0)
-        nc.scalar.activation(out=warm[:], in_=warm[:], func=ACT.Exp)
+
         nc.sync.dma_start(piece_list[:], offs)
         nc.sync.dma_start(
             out=store_bytes[:].bitcast(I32),
-            in_=piece_scales[0].bitcast(I32).unsqueeze(1).to_broadcast([16, 8, T // 4]),
+            in_=piece_scales[0].bitcast(I32).unsqueeze(1).to_broadcast([BLOCKS, BLOCK_PARTITIONS, T // 4]),
         )
         nc.sync.dma_start(out=query_raw[:], in_=query.rearrange("(p t) q -> p t q", t=PACK))
         for h in range(2):
             nc.sync.dma_start(out=cent_raw[h][:], in_=cent_rows[:, :, h * HALF : (h + 1) * HALF])
         nc.sync.dma_start(value_list[:], offs3)
         nc.sync.dma_start(base_list[:], offs2)
-        nc.sync.dma_start(out=vals_raw[0][:], in_=vals_rows[:, 0, :])
-        nc.sync.dma_start(out=vals_raw[1][:], in_=vals_rows[:, 1, :])
+        for j in range(EARLY_PLANES):
+            nc.sync.dma_start(out=vals_raw[j][:], in_=vals_rows[:, j, :])
         nc.sync.dma_start(out=store_words[:], in_=piece_words[0].rearrange("p c t -> p (c t)").bitcast(I32))
 
         ident = tile([P, P], F32, "ident")
@@ -100,241 +107,212 @@ def tile_attend_compositebase_pl_kernel(
         query_grouped = tile([P, Q, PACK], BF16, "query_grouped")
         query_codes = tile([P, Q], U32, "query_codes")
         query_scales = tile([P, Q], U8, "query_scales")
-        value_grouped = {}
-        value_codes = {}
         value_scales = [tile([P, P], U8, "value_scales%d" % j) for j in range(PACK)]
         result_codes = tile([P, Q], U32, "result_codes")
         result_scales = tile([P, Q], U8, "result_scales")
         out_rows = out_0.rearrange("(p j) q -> p j q", j=PACK)
         out_words = out_1[0].rearrange("p c t -> p (c t)").bitcast(I32)
-        t = {}
-        copy_on = {"V": nc.vector.tensor_copy, "S": nc.scalar.copy}
 
-        def qcols(c):
-            return slice(c * P, (c + 1) * P)
+        vals_half, picked_vals, value_bank, value_grouped, value_codes = {}, {}, {}, {}, {}
+        base_bank, picked_base, piece_bank, scores, neg_max, probs, row_sum, inv_sum = {}, {}, {}, {}, {}, {}, {}, {}
+        weight_rows, weight_bank, weight_grouped, weight_codes, weight_scales = {}, {}, {}, {}, {}
+        result_bank, result_grouped = {}, {}
 
-        def gby():
-            nc.vector.tensor_copy(picked_bytes[:], store_bytes[:].indirect(piece_list[:]))
+        def turn_pairs(bank, rows):
+            pairs = rows.bitcast(F32)
+            for u in range(2):
+                nc.tensor.transpose(bank[:, u, :], pairs[:, u::2], ident[:])
 
-        def mv():
-            for x in range(4):
-                nc.sync.dma_start(
-                    out=key_scales[32 * x : 32 * x + 4, :].bitcast(I32),
-                    in_=picked_bytes[32 * x : 32 * x + 32 : 8, :].bitcast(I32),
-                )
+        def group_pairs(grouped, bank):
+            nc.scalar.copy(
+                out=grouped.rearrange("s r t -> s (r t)").bitcast(F32).rearrange("s (r u) -> s r u", u=2),
+                in_=bank.rearrange("s u r -> s r u"),
+            )
 
-        def ts():
-            t["size_bank"] = ps.tile([P, PACK, P], F32, name="size_bank", tag="base01")
-            for k in range(PACK):
-                nc.tensor.transpose(t["size_bank"][:, k, :], size_cols[:, k : k + 1].to_broadcast([P, P]), ident[:])
-
-        def cq():
-            interleave(nc.vector.tensor_copy, query_grouped[:], query_raw[:])
-
-        def qq():
-            quantize(query_codes[:], query_scales[:], query_grouped[:])
-
-        def ccv(h):
-            interleave(nc.vector.tensor_copy, cent_grouped[h][:], cent_raw[h][:])
-
-        def qc(h):
-            quantize(cent_codes[h][:], cent_scales[h][:], cent_grouped[h][:])
-
-        def lv(j):
+        def load_plane(j):
             vals_raw[j] = tile([P, V], F32, "vals_raw%d" % j, "raw%d" % j)
             nc.sync.dma_start(out=vals_raw[j][:], in_=vals_rows[:, j, :])
 
-        def mb(c, h):
-            t["b", c, h] = ps.tile([P, HALF], F32, name="base_bank%d%d" % (c, h), tag="base%d%d" % (c, h))
-            product(t["b", c, h][:], query_codes[:, qcols(c)], query_scales[:, qcols(c)], cent_codes[h][:], cent_scales[h][:])
+        def multiply_bases(c, h):
+            base_bank[c, h] = ps.tile([P, HALF], F32, name="base_bank%d%d" % (c, h), tag="base%d%d" % (c, h))
+            cols = query_columns(c)
+            product(base_bank[c, h][:], query_codes[:, cols], query_scales[:, cols], cent_codes[h][:], cent_scales[h][:])
 
-        def cb(c, h):
-            nc.scalar.copy(out=base_scores[c][:, h * HALF : (h + 1) * HALF], in_=t["b", c, h][:])
+        def keep_bases(c, h):
+            nc.scalar.copy(out=base_scores[c][:, h * HALF : (h + 1) * HALF], in_=base_bank[c, h][:])
 
-        def gv(j, tag=None):
-            t["pv", j] = tile([P, SLOTS], BF16, "picked_vals%d" % j, tag)
-            nc.vector.tensor_copy(t["pv", j][:], vals_raw[j][:].indirect(value_list[:]))
+        def gather_plane_on_vector(j, after):
+            picked_vals[j] = tile([P, SLOTS], BF16, "picked_vals%d" % j, after)
+            nc.vector.tensor_copy(picked_vals[j][:], vals_raw[j][:].indirect(value_list[:]))
 
-        def cv(j, tag=None):
-            t["vh", j] = tile([P, V], BF16, "vals_half%d" % j, tag)
-            nc.scalar.activation(out=t["vh", j][:], in_=vals_raw[j][:], func=ACT.Copy)
+        def round_plane_on_scalar(j, after=None):
+            vals_half[j] = tile([P, V], BF16, "vals_half%d" % j, after)
+            nc.scalar.activation(out=vals_half[j][:], in_=vals_raw[j][:], func=ACT.Copy)
 
-        def sv(j, tag=None):
-            t["pv", j] = tile([P, SLOTS], BF16, "picked_vals%d" % j, tag)
-            nc.scalar.activation(out=t["pv", j][:], in_=t["vh", j][:].indirect(value_list[:]), func=ACT.Copy)
+        def gather_plane_on_scalar(j, after=None):
+            picked_vals[j] = tile([P, SLOTS], BF16, "picked_vals%d" % j, after)
+            nc.scalar.activation(out=picked_vals[j][:], in_=vals_half[j][:].indirect(value_list[:]), func=ACT.Copy)
 
-        def tv(j):
-            t["vb", j] = ps.tile([P, 2, P], F32, name="value_bank%d" % j, tag=["weight0", "base11", "piece0", "piece1"][j])
-            pairs = t["pv", j][:].bitcast(F32)
-            for u in range(2):
-                nc.tensor.transpose(t["vb", j][:, u, :], pairs[:, u::2], ident[:])
+        def turn_plane(j):
+            value_bank[j] = ps.tile([P, 2, P], F32, name="value_bank%d" % j, tag=VALUE_BANK_TAGS[j])
+            turn_pairs(value_bank[j], picked_vals[j][:])
 
-        def xv(j, e, tag=None):
-            value_grouped[j] = tile([P, P, PACK], BF16, "value_grouped%d" % j, tag)
-            copy_on[e](
-                out=value_grouped[j][:].rearrange("s c t -> s (c t)").bitcast(F32).rearrange("s (p u) -> s p u", u=2),
-                in_=t["vb", j][:].rearrange("s u p -> s p u"),
-            )
+        def group_plane(j, after=None):
+            value_grouped[j] = tile([P, P, PACK], BF16, "value_grouped%d" % j, after)
+            group_pairs(value_grouped[j][:], value_bank[j][:])
 
-        def qv(j, tag=None):
-            value_codes[j] = tile([P, P], U32, "value_codes%d" % j, tag)
+        def quantize_plane(j, after):
+            value_codes[j] = tile([P, P], U32, "value_codes%d" % j, after)
             quantize(value_codes[j][:], value_scales[j][:], value_grouped[j][:])
 
-        def gw(tag=None):
-            t["key_codes"] = tile([P, SLOTS], U32, "key_codes", tag)
-            nc.vector.tensor_copy(t["key_codes"][:], store_words[:].bitcast(U32).indirect(piece_list[:]))
+        def gather_bases(c, after):
+            picked_base[c] = tile([P, SLOTS], F32, "picked_base%d" % c, after)
+            nc.vector.tensor_copy(picked_base[c][:], base_scores[c][:].indirect(base_list[:]))
 
-        def ma(c):
-            t["a", c] = ps.tile([P, SLOTS], F32, name="piece_bank%d" % c, tag="piece%d" % c)
-            product(t["a", c][:], query_codes[:, qcols(c)], query_scales[:, qcols(c)], t["key_codes"][:], key_scales[:])
+        def multiply_pieces(c, key_codes):
+            piece_bank[c] = ps.tile([P, SLOTS], F32, name="piece_bank%d" % c, tag="piece%d" % c)
+            cols = query_columns(c)
+            product(piece_bank[c][:], query_codes[:, cols], query_scales[:, cols], key_codes[:], key_scales[:])
 
-        def gb(c, tag=None):
-            t["g", c] = tile([P, SLOTS], F32, "picked_base%d" % c, tag)
-            nc.vector.tensor_copy(t["g", c][:], base_scores[c][:].indirect(base_list[:]))
-
-        def s(c):
-            t["s", c] = tile([P, SLOTS], F32, "scores%d" % c)
+        def add_scores(c):
+            scores[c] = tile([P, SLOTS], F32, "scores%d" % c)
             nc.vector.scalar_tensor_tensor(
-                out=t["s", c][:], in0=t["g", c][:], scalar=trust_cols[:, c : c + 1], in1=t["a", c][:],
+                out=scores[c][:], in0=picked_base[c][:], scalar=trust_cols[:, c : c + 1], in1=piece_bank[c][:],
                 op0=ALU.mult, op1=ALU.add,
             )
 
-        def m(c, tag=None):
-            t["m", c] = tile([P, 1], F32, "neg_max%d" % c, tag)
-            nc.vector.tensor_reduce(out=t["m", c][:], in_=t["s", c][:], axis=AXIS.X, op=ALU.max, negate=True)
+        def row_maximum(c):
+            neg_max[c] = tile([P, 1], F32, "neg_max%d" % c)
+            nc.vector.tensor_reduce(out=neg_max[c][:], in_=scores[c][:], axis=AXIS.X, op=ALU.max, negate=True)
 
-        def e(c, tag=None):
-            t["p", c] = tile([P, SLOTS], F32, "probs%d" % c, tag)
-            t["sum", c] = tile([P, 1], F32, "row_sum%d" % c)
-            nc.scalar.activation(out=t["p", c][:], in_=t["s", c][:], func=ACT.Exp, bias=t["m", c][:], accum_out=t["sum", c][:])
+        def exponentials(c, after=None):
+            probs[c] = tile([P, SLOTS], F32, "probs%d" % c, after)
+            row_sum[c] = tile([P, 1], F32, "row_sum%d" % c)
+            nc.scalar.activation(
+                out=probs[c][:], in_=scores[c][:], func=ACT.Exp, bias=neg_max[c][:], accum_out=row_sum[c][:]
+            )
 
-        def r(c, tag=None):
-            t["r", c] = tile([P, 1], F32, "inv_sum%d" % c, tag)
-            nc.vector.reciprocal(out=t["r", c][:], in_=t["sum", c][:])
+        def invert_sum(c, after=None):
+            inv_sum[c] = tile([P, 1], F32, "inv_sum%d" % c, after)
+            nc.vector.reciprocal(out=inv_sum[c][:], in_=row_sum[c][:])
 
-        def w(c):
-            t["w", c] = tile([P, SLOTS], BF16, "w_rows%d" % c)
+        def weigh(c, size_bank):
+            weight_rows[c] = tile([P, SLOTS], BF16, "w_rows%d" % c)
             nc.vector.scalar_tensor_tensor(
-                out=t["w", c][:].rearrange("q (s t) -> q s t", t=PACK),
-                in0=t["p", c][:].rearrange("q (s t) -> q s t", t=PACK),
-                scalar=t["r", c][:],
-                in1=t["size_bank"][:].rearrange("q t s -> q s t"),
+                out=weight_rows[c][:].rearrange("q (s t) -> q s t", t=PACK),
+                in0=probs[c][:].rearrange("q (s t) -> q s t", t=PACK),
+                scalar=inv_sum[c][:],
+                in1=size_bank[:].rearrange("q t s -> q s t"),
                 op0=ALU.mult, op1=ALU.mult,
             )
 
-        def tw(c):
-            t["wb", c] = ps.tile([P, 2, P], F32, name="weight_bank%d" % c, tag="weight%d" % c)
-            pairs = t["w", c][:].bitcast(F32)
-            for u in range(2):
-                nc.tensor.transpose(t["wb", c][:, u, :], pairs[:, u::2], ident[:])
+        def turn_weights(c):
+            weight_bank[c] = ps.tile([P, 2, P], F32, name="weight_bank%d" % c, tag="weight%d" % c)
+            turn_pairs(weight_bank[c], weight_rows[c][:])
 
-        def cw(c, e):
-            t["wg", c] = tile([P, P, PACK], BF16, "weight_grouped%d" % c)
-            copy_on[e](
-                out=t["wg", c][:].rearrange("s q t -> s (q t)").bitcast(F32).rearrange("s (q u) -> s q u", u=2),
-                in_=t["wb", c][:].rearrange("s u q -> s q u"),
+        def group_weights(c):
+            weight_grouped[c] = tile([P, P, PACK], BF16, "weight_grouped%d" % c)
+            group_pairs(weight_grouped[c][:], weight_bank[c][:])
+
+        def quantize_weights(c):
+            weight_codes[c] = tile([P, P], U32, "weight_codes%d" % c)
+            weight_scales[c] = tile([P, P], U8, "weight_scales%d" % c)
+            quantize(weight_codes[c][:], weight_scales[c][:], weight_grouped[c][:])
+
+        def multiply_values(c):
+            result_bank[c] = ps.tile([P, PACK, P], F32, name="result_bank%d" % c, tag="base%d0" % c)
+            for j in range(PACK):
+                product(result_bank[c][:, j, :], value_codes[j][:], value_scales[j][:], weight_codes[c][:], weight_scales[c][:])
+
+        def hand_out(c, float_copy):
+            cols = query_columns(c)
+            result_grouped[c] = tile([P, P, PACK], BF16, "result_grouped%d" % c)
+            nc.vector.tensor_copy(out=result_grouped[c][:], in_=result_bank[c][:].rearrange("p j q -> p q j"))
+            result = tile([P, PACK, P], F32, "result%d" % c)
+            float_copy(out=result[:], in_=result_bank[c][:])
+            nc.sync.dma_start(out=out_rows[:, :, cols], in_=result[:])
+            quantize(result_codes[:, cols], result_scales[:, cols], result_grouped[c][:])
+            nc.sync.dma_start(out=out_words[:, cols], in_=result_codes[:, cols].bitcast(I32))
+
+        nc.vector.tensor_copy(picked_bytes[:], store_bytes[:].indirect(piece_list[:]))
+        for x in range(P // QUADRANT):
+            first = QUADRANT * x
+            nc.sync.dma_start(
+                out=key_scales[first : first + PACK, :].bitcast(I32),
+                in_=picked_bytes[first : first + QUADRANT : BLOCK_PARTITIONS, :].bitcast(I32),
             )
 
-        def qw(c):
-            t["wc", c] = tile([P, P], U32, "weight_codes%d" % c)
-            t["ws", c] = tile([P, P], U8, "weight_scales%d" % c)
-            quantize(t["wc", c][:], t["ws", c][:], t["wg", c][:])
+        round_and_group(query_grouped[:], query_raw[:])
+        load_plane(2)
+        quantize(query_codes[:], query_scales[:], query_grouped[:])
+        round_and_group(cent_grouped[0][:], cent_raw[0][:])
+        load_plane(3)
+        quantize(cent_codes[0][:], cent_scales[0][:], cent_grouped[0][:])
+        round_and_group(cent_grouped[1][:], cent_raw[1][:])
+        multiply_bases(0, 0)
+        multiply_bases(1, 0)
+        quantize(cent_codes[1][:], cent_scales[1][:], cent_grouped[1][:])
+        keep_bases(0, 0)
+        keep_bases(1, 0)
+        round_plane_on_scalar(0)
+        gather_plane_on_vector(1, after="cent_grouped1")
+        multiply_bases(0, 1)
+        multiply_bases(1, 1)
+        keep_bases(0, 1)
+        keep_bases(1, 1)
 
-        def mo(c, order):
-            if ("o", c) not in t:
-                t["o", c] = ps.tile([P, PACK, P], F32, name="result_bank%d" % c, tag="base%d0" % c)
-            for j in order:
-                product(t["o", c][:, j, :], value_codes[j][:], value_scales[j][:], t["wc", c][:], t["ws", c][:])
+        size_bank = ps.tile([P, PACK, P], F32, name="size_bank", tag="base01")
+        for t in range(PACK):
+            nc.tensor.transpose(size_bank[:, t, :], size_cols[:, t : t + 1].to_broadcast([P, P]), ident[:])
 
-        def ob(c, from_sbuf=False):
-            t["og", c] = tile([P, P, PACK], BF16, "result_grouped%d" % c)
-            if from_sbuf:
-                interleave(nc.vector.tensor_copy, t["og", c][:], t["res", c][:])
-            else:
-                nc.vector.tensor_copy(out=t["og", c][:], in_=t["o", c][:].rearrange("p j q -> p q j"))
+        gather_plane_on_scalar(0, after="cent_scales1")
+        gather_bases(0, after="vals_raw1")
+        turn_plane(1)
+        key_codes = tile([P, SLOTS], U32, "key_codes", "cent_codes1")
+        nc.vector.tensor_copy(key_codes[:], store_words[:].bitcast(U32).indirect(piece_list[:]))
+        group_plane(1)
+        turn_plane(0)
+        round_plane_on_scalar(2, after="vals_half0")
+        gather_bases(1, after="store_words")
+        multiply_pieces(0, key_codes)
+        group_plane(0)
+        multiply_pieces(1, key_codes)
+        gather_plane_on_scalar(2)
 
-        def of(c, e):
-            result = tile([P, PACK, P], F32, "result%d" % c)
-            t["res", c] = result
-            copy_on[e](out=result[:], in_=t["o", c][:])
-            nc.sync.dma_start(out=out_rows[:, :, qcols(c)], in_=result[:])
+        add_scores(0)
+        add_scores(1)
+        row_maximum(0)
+        turn_plane(2)
+        row_maximum(1)
+        exponentials(0, after="vals_half0")
+        gather_plane_on_vector(3, after="store_words")
+        exponentials(1)
+        group_plane(2, after="scores0")
+        invert_sum(0, after="raw3")
+        invert_sum(1)
+        turn_plane(3)
+        weigh(0, size_bank)
+        group_plane(3, after="scores1")
+        weigh(1, size_bank)
 
-        def qo(c):
-            quantize(result_codes[:, qcols(c)], result_scales[:, qcols(c)], t["og", c][:])
-            nc.sync.dma_start(out=out_words[:, qcols(c)], in_=result_codes[:, qcols(c)].bitcast(I32))
+        turn_weights(0)
+        quantize_plane(0, after="vals_half0")
+        quantize_plane(1, after="raw3")
+        group_weights(0)
+        turn_weights(1)
+        quantize_weights(0)
+        quantize_plane(2, after="probs1")
+        quantize_plane(3, after="inv_sum1")
+        group_weights(1)
+        multiply_values(0)
+        quantize_weights(1)
+        multiply_values(1)
 
-        def sw():
-            for x in range(4):
-                queue = nc.sync if x % 2 == 0 else nc.scalar
-                queue.dma_start(
-                    out=out_2[0, 4 * x : 4 * x + 4, :].bitcast(I32),
-                    in_=result_scales[32 * x : 32 * x + 4, :].bitcast(I32),
-                )
-
-        gby()
-        mv()
-        cq()
-        lv(2)
-        qq()
-        ccv(0)
-        lv(3)
-        qc(0)
-        ccv(1)
-        mb(0,0)
-        mb(1,0)
-        qc(1)
-        cb(0,0)
-        cb(1,0)
-        cv(0)
-        gv(1,"cent_grouped1")
-        mb(0,1)
-        mb(1,1)
-        cb(0,1)
-        cb(1,1)
-        ts()
-        sv(0,"cent_scales1")
-        gb(0,"vals_raw1")
-        tv(1)
-        gw("cent_codes1")
-        xv(1,"S")
-        tv(0)
-        cv(2,"vals_half0")
-        gb(1,"store_words")
-        ma(0)
-        xv(0,"S")
-        ma(1)
-        sv(2)
-        s(0)
-        s(1)
-        m(0)
-        tv(2)
-        m(1)
-        e(0,"vals_half0")
-        gv(3,"store_words")
-        e(1)
-        xv(2,"S","scores0")
-        r(0,"raw3")
-        r(1)
-        tv(3)
-        w(0)
-        xv(3,"S","scores1")
-        w(1)
-        tw(0)
-        qv(0,"vals_half0")
-        qv(1,"raw3")
-        cw(0,"S")
-        tw(1)
-        qw(0)
-        qv(2,"probs1")
-        qv(3,"inv_sum1")
-        cw(1,"S")
-        mo(0,[0,1,2,3])
-        qw(1)
-        mo(1,[0,1,2,3])
-        ob(0)
-        of(0,"S")
-        qo(0)
-        ob(1)
-        of(1,"V")
-        qo(1)
-        sw()
+        hand_out(0, nc.scalar.copy)
+        hand_out(1, nc.vector.tensor_copy)
+        for x in range(P // QUADRANT):
+            queue = nc.sync if x % 2 == 0 else nc.scalar
+            queue.dma_start(
+                out=out_2[0, PACK * x : PACK * (x + 1), :].bitcast(I32),
+                in_=result_scales[QUADRANT * x : QUADRANT * x + PACK, :].bitcast(I32),
+            )

from contextlib import ExitStack

import concourse.mybir as mybir
from concourse.masks import make_identity

F32 = mybir.dt.float32
BF16 = mybir.dt.bfloat16
I32 = mybir.dt.int32
U32 = mybir.dt.uint32
U16 = mybir.dt.uint16
U8 = mybir.dt.uint8
FP8X4 = mybir.dt.float8_e4m3fn_x4
ALU = mybir.AluOpType
ACT = mybir.ActivationFunctionType
AXIS = mybir.AxisListType

P = 128
PACK = 4
D, T, U, V, SLOTS, Q, E = 512, 2048, 512, 1024, 512, 256, 512
Q_TILES = Q // P
BLOCKS = D // 32
QUADRANT = 32
BLOCK_PARTITIONS = 8
LIST_COLUMNS = SLOTS // 16
BASE_WINDOW = 704
HALF = U // 2
EARLY_PLANES = 2
VALUE_BANK_TAGS = ("weight0", "base11", "piece0", "piece1")

FLOPS = 2 * Q * D * SLOTS + 2 * Q * D * U + 2 * E * SLOTS * Q


def query_columns(c):
    return slice(c * P, (c + 1) * P)


def tile_attend_compositebase_pl_kernel(
    tc, query, piece_words, piece_scales, cent, trust, size, vals, offs, offs2, offs3, out_0, out_1, out_2
):
    nc = tc.nc

    def round_and_group(grouped, raw):
        nc.vector.tensor_copy(
            out=grouped.rearrange("p (c i) t -> p c t i", i=PACK),
            in_=raw.rearrange("p t (c i) -> p c t i", i=PACK),
        )

    def quantize(codes, scales, grouped):
        nc.vector.quantize_mx(out=codes.bitcast(FP8X4), scales=scales, in_=grouped.rearrange("p c t -> p (c t)"))

    def product(out, lhs_codes, lhs_scales, rhs_codes, rhs_scales):
        nc.tensor.matmul_mx(
            out=out, lhsT=lhs_codes.bitcast(FP8X4), lhsT_scale=lhs_scales,
            rhs=rhs_codes.bitcast(FP8X4), rhs_scale=rhs_scales, start=True, stop=True,
        )

    with ExitStack() as ctx:
        sb = ctx.enter_context(tc.tile_pool(name="sb", bufs=1))
        ps = ctx.enter_context(tc.psum_pool(name="ps", bufs=1))

        def tile(shape, dtype, name, after=None):
            return sb.tile(shape, dtype, name=name, tag=after or name, align_bytes=64)

        piece_list = sb.tile([P, LIST_COLUMNS], U16, name="piece_list")
        base_list = sb.tile([P, LIST_COLUMNS], U16, name="base_list")
        value_list = sb.tile([P, LIST_COLUMNS], U16, name="value_list")
        store_bytes = tile([P, T], U8, "store_bytes")
        store_words = tile([P, T], I32, "store_words")
        query_raw = tile([P, PACK, Q], F32, "query_raw", "raw2")
        cent_raw = [tile([P, PACK, HALF], F32, "cent_raw%d" % h, tag) for h, tag in enumerate(("raw3", "raw4"))]
        vals_raw = {j: tile([P, V], F32, "vals_raw%d" % j) for j in range(EARLY_PLANES)}
        trust_cols = tile([P, Q_TILES], F32, "trust_cols")
        size_cols = tile([P, PACK], F32, "size_cols")
        cent_rows = cent.rearrange("(p t) u -> p t u", t=PACK)
        vals_rows = vals.rearrange("(p j) v -> p j v", j=PACK)

        nc.scalar.dma_start(out=size_cols[:], in_=size.rearrange("o (p t) -> p (o t)", t=PACK))
        with nc.allow_non_contiguous_dma(reason="one trust value a partition and query tile"):
            nc.scalar.dma_start(out=trust_cols[:], in_=trust.rearrange("(c p) o -> p (c o)", p=P))

        nc.sync.dma_start(piece_list[:], offs)
        nc.sync.dma_start(
            out=store_bytes[:].bitcast(I32),
            in_=piece_scales[0].bitcast(I32).unsqueeze(1).to_broadcast([BLOCKS, BLOCK_PARTITIONS, T // 4]),
        )
        nc.sync.dma_start(out=query_raw[:], in_=query.rearrange("(p t) q -> p t q", t=PACK))
        for h in range(2):
            nc.sync.dma_start(out=cent_raw[h][:], in_=cent_rows[:, :, h * HALF : (h + 1) * HALF])
        nc.sync.dma_start(value_list[:], offs3)
        nc.sync.dma_start(base_list[:], offs2)
        for j in range(EARLY_PLANES):
            nc.sync.dma_start(out=vals_raw[j][:], in_=vals_rows[:, j, :])
        nc.sync.dma_start(out=store_words[:], in_=piece_words[0].rearrange("p c t -> p (c t)").bitcast(I32))

        ident = tile([P, P], F32, "ident")
        make_identity(nc, ident[:])
        key_scales = tile([P, SLOTS], U8, "key_scales")
        nc.gpsimd.memset(key_scales[:].bitcast(I32), 0)
        base_scores = [tile([P, BASE_WINDOW], F32, "base_scores%d" % c) for c in range(Q_TILES)]
        for c in range(Q_TILES):
            nc.gpsimd.memset(base_scores[c][:, U:], 0.0)

        picked_bytes = tile([P, SLOTS], U8, "picked_bytes")
        cent_codes = [tile([P, HALF], U32, "cent_codes%d" % h) for h in range(2)]
        cent_scales = [tile([P, HALF], U8, "cent_scales%d" % h) for h in range(2)]
        cent_grouped = [tile([P, HALF, PACK], BF16, "cent_grouped%d" % h) for h in range(2)]
        query_grouped = tile([P, Q, PACK], BF16, "query_grouped")
        query_codes = tile([P, Q], U32, "query_codes")
        query_scales = tile([P, Q], U8, "query_scales")
        value_scales = [tile([P, P], U8, "value_scales%d" % j) for j in range(PACK)]
        result_codes = tile([P, Q], U32, "result_codes")
        result_scales = tile([P, Q], U8, "result_scales")
        out_rows = out_0.rearrange("(p j) q -> p j q", j=PACK)
        out_words = out_1[0].rearrange("p c t -> p (c t)").bitcast(I32)

        vals_half, picked_vals, value_bank, value_grouped, value_codes = {}, {}, {}, {}, {}
        base_bank, picked_base, piece_bank, scores, neg_max, probs, row_sum, inv_sum = {}, {}, {}, {}, {}, {}, {}, {}
        weight_rows, weight_bank, weight_grouped, weight_codes, weight_scales = {}, {}, {}, {}, {}
        result_bank, result_grouped = {}, {}

        def turn_pairs(bank, rows):
            pairs = rows.bitcast(F32)
            for u in range(2):
                nc.tensor.transpose(bank[:, u, :], pairs[:, u::2], ident[:])

        def group_pairs(grouped, bank):
            nc.scalar.copy(
                out=grouped.rearrange("s r t -> s (r t)").bitcast(F32).rearrange("s (r u) -> s r u", u=2),
                in_=bank.rearrange("s u r -> s r u"),
            )

        def load_plane(j):
            vals_raw[j] = tile([P, V], F32, "vals_raw%d" % j, "raw%d" % j)
            nc.sync.dma_start(out=vals_raw[j][:], in_=vals_rows[:, j, :])

        def multiply_bases(c, h):
            base_bank[c, h] = ps.tile([P, HALF], F32, name="base_bank%d%d" % (c, h), tag="base%d%d" % (c, h))
            cols = query_columns(c)
            product(base_bank[c, h][:], query_codes[:, cols], query_scales[:, cols], cent_codes[h][:], cent_scales[h][:])

        def keep_bases(c, h):
            nc.scalar.copy(out=base_scores[c][:, h * HALF : (h + 1) * HALF], in_=base_bank[c, h][:])

        def gather_plane_on_vector(j, after):
            picked_vals[j] = tile([P, SLOTS], BF16, "picked_vals%d" % j, after)
            nc.vector.tensor_copy(picked_vals[j][:], vals_raw[j][:].indirect(value_list[:]))

        def round_plane_on_scalar(j, after=None):
            vals_half[j] = tile([P, V], BF16, "vals_half%d" % j, after)
            nc.scalar.activation(out=vals_half[j][:], in_=vals_raw[j][:], func=ACT.Copy)

        def gather_plane_on_scalar(j, after=None):
            picked_vals[j] = tile([P, SLOTS], BF16, "picked_vals%d" % j, after)
            nc.scalar.activation(out=picked_vals[j][:], in_=vals_half[j][:].indirect(value_list[:]), func=ACT.Copy)

        def turn_plane(j):
            value_bank[j] = ps.tile([P, 2, P], F32, name="value_bank%d" % j, tag=VALUE_BANK_TAGS[j])
            turn_pairs(value_bank[j], picked_vals[j][:])

        def group_plane(j, after=None):
            value_grouped[j] = tile([P, P, PACK], BF16, "value_grouped%d" % j, after)
            group_pairs(value_grouped[j][:], value_bank[j][:])

        def quantize_plane(j, after):
            value_codes[j] = tile([P, P], U32, "value_codes%d" % j, after)
            quantize(value_codes[j][:], value_scales[j][:], value_grouped[j][:])

        def gather_bases(c, after):
            picked_base[c] = tile([P, SLOTS], F32, "picked_base%d" % c, after)
            nc.vector.tensor_copy(picked_base[c][:], base_scores[c][:].indirect(base_list[:]))

        def multiply_pieces(c, key_codes):
            piece_bank[c] = ps.tile([P, SLOTS], F32, name="piece_bank%d" % c, tag="piece%d" % c)
            cols = query_columns(c)
            product(piece_bank[c][:], query_codes[:, cols], query_scales[:, cols], key_codes[:], key_scales[:])

        def add_scores(c):
            scores[c] = tile([P, SLOTS], F32, "scores%d" % c)
            nc.vector.scalar_tensor_tensor(
                out=scores[c][:], in0=picked_base[c][:], scalar=trust_cols[:, c : c + 1], in1=piece_bank[c][:],
                op0=ALU.mult, op1=ALU.add,
            )

        def row_maximum(c):
            neg_max[c] = tile([P, 1], F32, "neg_max%d" % c)
            nc.vector.tensor_reduce(out=neg_max[c][:], in_=scores[c][:], axis=AXIS.X, op=ALU.max, negate=True)

        def exponentials(c, after=None):
            probs[c] = tile([P, SLOTS], F32, "probs%d" % c, after)
            row_sum[c] = tile([P, 1], F32, "row_sum%d" % c)
            nc.scalar.activation(
                out=probs[c][:], in_=scores[c][:], func=ACT.Exp, bias=neg_max[c][:], accum_out=row_sum[c][:]
            )

        def invert_sum(c, after=None):
            inv_sum[c] = tile([P, 1], F32, "inv_sum%d" % c, after)
            nc.vector.reciprocal(out=inv_sum[c][:], in_=row_sum[c][:])

        def weigh(c, size_bank):
            weight_rows[c] = tile([P, SLOTS], BF16, "w_rows%d" % c)
            nc.vector.scalar_tensor_tensor(
                out=weight_rows[c][:].rearrange("q (s t) -> q s t", t=PACK),
                in0=probs[c][:].rearrange("q (s t) -> q s t", t=PACK),
                scalar=inv_sum[c][:],
                in1=size_bank[:].rearrange("q t s -> q s t"),
                op0=ALU.mult, op1=ALU.mult,
            )

        def turn_weights(c):
            weight_bank[c] = ps.tile([P, 2, P], F32, name="weight_bank%d" % c, tag="weight%d" % c)
            turn_pairs(weight_bank[c], weight_rows[c][:])

        def group_weights(c):
            weight_grouped[c] = tile([P, P, PACK], BF16, "weight_grouped%d" % c)
            group_pairs(weight_grouped[c][:], weight_bank[c][:])

        def quantize_weights(c):
            weight_codes[c] = tile([P, P], U32, "weight_codes%d" % c)
            weight_scales[c] = tile([P, P], U8, "weight_scales%d" % c)
            quantize(weight_codes[c][:], weight_scales[c][:], weight_grouped[c][:])

        def multiply_values(c):
            result_bank[c] = ps.tile([P, PACK, P], F32, name="result_bank%d" % c, tag="base%d0" % c)
            for j in range(PACK):
                product(result_bank[c][:, j, :], value_codes[j][:], value_scales[j][:], weight_codes[c][:], weight_scales[c][:])

        def hand_out(c, float_copy):
            cols = query_columns(c)
            result_grouped[c] = tile([P, P, PACK], BF16, "result_grouped%d" % c)
            nc.vector.tensor_copy(out=result_grouped[c][:], in_=result_bank[c][:].rearrange("p j q -> p q j"))
            result = tile([P, PACK, P], F32, "result%d" % c)
            float_copy(out=result[:], in_=result_bank[c][:])
            nc.sync.dma_start(out=out_rows[:, :, cols], in_=result[:])
            quantize(result_codes[:, cols], result_scales[:, cols], result_grouped[c][:])
            nc.sync.dma_start(out=out_words[:, cols], in_=result_codes[:, cols].bitcast(I32))

        nc.vector.tensor_copy(picked_bytes[:], store_bytes[:].indirect(piece_list[:]))
        for x in range(P // QUADRANT):
            first = QUADRANT * x
            nc.sync.dma_start(
                out=key_scales[first : first + PACK, :].bitcast(I32),
                in_=picked_bytes[first : first + QUADRANT : BLOCK_PARTITIONS, :].bitcast(I32),
            )

        round_and_group(query_grouped[:], query_raw[:])
        load_plane(2)
        quantize(query_codes[:], query_scales[:], query_grouped[:])
        round_and_group(cent_grouped[0][:], cent_raw[0][:])
        load_plane(3)
        quantize(cent_codes[0][:], cent_scales[0][:], cent_grouped[0][:])
        round_and_group(cent_grouped[1][:], cent_raw[1][:])
        multiply_bases(0, 0)
        multiply_bases(1, 0)
        quantize(cent_codes[1][:], cent_scales[1][:], cent_grouped[1][:])
        keep_bases(0, 0)
        keep_bases(1, 0)
        round_plane_on_scalar(0)
        gather_plane_on_vector(1, after="cent_grouped1")
        multiply_bases(0, 1)
        multiply_bases(1, 1)
        keep_bases(0, 1)
        keep_bases(1, 1)

        size_bank = ps.tile([P, PACK, P], F32, name="size_bank", tag="base01")
        for t in range(PACK):
            nc.tensor.transpose(size_bank[:, t, :], size_cols[:, t : t + 1].to_broadcast([P, P]), ident[:])

        gather_plane_on_scalar(0, after="cent_scales1")
        gather_bases(0, after="vals_raw1")
        turn_plane(1)
        key_codes = tile([P, SLOTS], U32, "key_codes", "cent_codes1")
        nc.vector.tensor_copy(key_codes[:], store_words[:].bitcast(U32).indirect(piece_list[:]))
        group_plane(1)
        turn_plane(0)
        round_plane_on_scalar(2, after="vals_half0")
        gather_bases(1, after="store_words")
        multiply_pieces(0, key_codes)
        group_plane(0)
        multiply_pieces(1, key_codes)
        gather_plane_on_scalar(2)

        add_scores(0)
        add_scores(1)
        row_maximum(0)
        turn_plane(2)
        row_maximum(1)
        exponentials(0, after="vals_half0")
        gather_plane_on_vector(3, after="store_words")
        exponentials(1)
        group_plane(2, after="scores0")
        invert_sum(0, after="raw3")
        invert_sum(1)
        turn_plane(3)
        weigh(0, size_bank)
        group_plane(3, after="scores1")
        weigh(1, size_bank)

        turn_weights(0)
        quantize_plane(0, after="vals_half0")
        quantize_plane(1, after="raw3")
        group_weights(0)
        turn_weights(1)
        quantize_weights(0)
        quantize_plane(2, after="probs1")
        quantize_plane(3, after="inv_sum1")
        group_weights(1)
        multiply_values(0)
        quantize_weights(1)
        multiply_values(1)

        hand_out(0, nc.scalar.copy)
        hand_out(1, nc.vector.tensor_copy)
        for x in range(P // QUADRANT):
            queue = nc.sync if x % 2 == 0 else nc.scalar
            queue.dma_start(
                out=out_2[0, PACK * x : PACK * (x + 1), :].bitcast(I32),
                in_=result_scales[QUADRANT * x : QUADRANT * x + PACK, :].bitcast(I32),
            )
